import numpy as np, ml_dtypes
CORES = [211,219,227,235,243,251,83,91,99,107,115,123]
N = 12
CB = 3
def setup_inputs(rng):
    k = (rng.standard_normal((N, 128, CB * 128), dtype=np.float32) / 8).astype(ml_dtypes.bfloat16)
    kt = np.concatenate([k[:, :, 128 * c:128 * c + 128].transpose(0, 2, 1) for c in range(CB)], axis=2)
    tri = np.triu(np.ones((128, 128), np.float32)).astype(ml_dtypes.bfloat16)
    return {"q": (rng.standard_normal((N, 128, CB * 128), dtype=np.float32) / 8).astype(ml_dtypes.bfloat16), "k": k, "kt": kt, "v": rng.standard_normal((N, 128, CB * 128), dtype=np.float32).astype(ml_dtypes.bfloat16), "m": np.broadcast_to(tri, (N, 128, 128)).copy()}
def setup_inputs_big(rng):
    d = setup_inputs(rng)
    for k in ("q", "k", "kt", "v"): d[k] = (d[k].astype(np.float32) * 1024.0).astype(d[k].dtype)
    return d
def setup_inputs_small(rng):
    d = setup_inputs(rng)
    for k in ("q", "k", "kt", "v"): d[k] = (d[k].astype(np.float32) * (1 / 1024.0)).astype(d[k].dtype)
    return d
def setup_inputs_apart(rng):
    d = setup_inputs(rng)
    f = (10.0 ** rng.permutation(np.linspace(-1.5, 1.5, N))).astype(np.float32).reshape(N, 1, 1)
    for k in ("q", "k", "kt", "v"): d[k] = (d[k].astype(np.float32) * f).astype(d[k].dtype)
    return d
def reference(q, k, kt, v, m):
    Q, K, KT, V, M = q.astype(np.float64), k.astype(np.float64), kt.astype(np.float64), v.astype(np.float64), m.astype(np.float64)
    y = np.zeros((N, 128, CB * 128)); Z = np.zeros((128, 128))
    for r in range(N):
        for c in range(CB):
            s = slice(128 * c, 128 * c + 128)
            y[r][:, s] = Z.T @ Q[r][:, s] + V[r][:, s].T @ ((K[r][:, s].T @ Q[r][:, s]) * M[r])
            Z = Z + KT[r][:, s].T @ V[r][:, s]
    return {"y": y.astype(ml_dtypes.bfloat16)}

@@ -1,0 +1,158 @@
+from concourse.bass import DstId, RemoteDMATransfer
+from concourse.mybir import AluOpType
+
+N, CB, B = 12, 3, 128
+W = CB * B
+GS = 4
+NG = N // GS
+NLAND = GS + NG - 1
+
+SCRATCH = {
+    "kt_sb": ("sbuf", [B, W], "bfloat16"),
+    "v_sb": ("sbuf", [B, W], "bfloat16"),
+    "q_sb": ("sbuf", [B, W], "bfloat16"),
+    "k_sb": ("sbuf", [B, W], "bfloat16"),
+    "m_sb": ("sbuf", [B, B], "bfloat16"),
+    "s_sb": ("sbuf", [B, B], "bfloat16"),
+    "l_sb": ("sbuf", [B, 2 * B], "bfloat16"),
+    "wm_sb": ("sbuf", [B, W], "bfloat16"),
+    "yl_sb": ("sbuf", [B, W], "float32"),
+    "y_sb": ("sbuf", [B, W], "bfloat16"),
+    "ps_s": ("psum", [B, 512], "float32"),
+    "ps_l": ("psum", [B, 512], "float32"),
+    "ps_w": ("psum", [B, 512], "float32"),
+    "ps_y": ("psum", [B, 512], "float32"),
+    "ps_z": ("psum", [B, 512], "float32"),
+}
+for _i in range(NLAND):
+    SCRATCH["land%d" % _i] = ("sbuf", [B, B], "bfloat16")
+
+SEMAPHORES = ["ld_kt", "ld_v", "ld_q", "ld_k", "ld_m", "mm_s", "mm_l", "mm_w", "mm_y", "mm_z",
+              "s_rdy", "l_rdy", "wm_rdy", "yl_rdy", "y_rdy", "sent", "stored"] + ["arr%d" % _i for _i in range(NLAND)]
+
+
+def plan(cores, topo):
+    calls = [[] for _ in range(N)]
+    pieces = [[] for _ in range(N)]
+    for j in range(NG):
+        mem = list(range(j * GS, (j + 1) * GS))
+        later = list(range((j + 1) * GS, N))
+        share = {r: [] for r in mem}
+        for d in later:
+            own = [r for r in mem if topo.same_plane(cores[r], cores[d])]
+            cand = own if own else [r for r in mem if topo.may_write(cores[r], cores[d])]
+            share[min(cand, key=lambda r: len(share[r]))].append(d)
+        for i, r in enumerate(mem):
+            dst = [mem[(i + t) % GS] for t in range(1, GS)]
+            dst = [d for d in dst if d > r or share[d]]
+            if dst:
+                calls[r].append(([], dst, i))
+            if share[r]:
+                calls[r].append(([p for p in range(GS) if p != i], share[r], GS + j))
+            pieces[r] = [p for p in range(i - 1, -1, -1)] + [GS + jj for jj in range(j - 1, -1, -1)]
+    return calls, pieces
+
+
+def rank_program(g, core, T, topo):
+    rank = T.rank_of(core)
+    if rank is None:
+        return
+    cores = T.cores
+    calls, pieces = plan(cores, topo)
+    mine, zp = calls[rank], pieces[rank]
+    sem = T.sem
+    te, ve, sy, sc = g.tensor, g.vector, g.sync, g.scalar
+    blk = [slice(B * c, B * c + B) for c in range(CB)]
+
+    sy.dma_start(T.kt_sb[:], T.kt[:]).then_inc(sem.ld_kt, 16)
+    sc.dma_start(T.v_sb[:], T.v[:]).then_inc(sem.ld_v, 16)
+    sy.dma_start(T.q_sb[:], T.q[:]).then_inc(sem.ld_q, 16)
+    sc.dma_start(T.k_sb[:], T.k[:]).then_inc(sem.ld_k, 16)
+    sy.dma_start(T.m_sb[:], T.m[:]).then_inc(sem.ld_m, 16)
+
+    te.wait_ge(sem.ld_kt, 16)
+    te.wait_ge(sem.ld_v, 16)
+    if mine:
+        for c in range(CB):
+            te.matmul(T.ps_s[:, 0:B], T.kt_sb[:, blk[c]], T.v_sb[:, blk[c]], c == 0, c == CB - 1).then_inc(sem.mm_s, 1)
+    te.matmul(T.ps_l[:, 0:B], T.kt_sb[:, blk[0]], T.v_sb[:, blk[0]], True, True).then_inc(sem.mm_l, 1)
+    te.matmul(T.ps_l[:, B:2 * B], T.kt_sb[:, blk[0]], T.v_sb[:, blk[0]], True, False).then_inc(sem.mm_l, 1)
+    te.matmul(T.ps_l[:, B:2 * B], T.kt_sb[:, blk[1]], T.v_sb[:, blk[1]], False, True).then_inc(sem.mm_l, 1)
+    te.wait_ge(sem.ld_q, 16)
+    te.wait_ge(sem.ld_k, 16)
+    for c in range(CB):
+        te.matmul(T.ps_w[:, blk[c]], T.k_sb[:, blk[c]], T.q_sb[:, blk[c]], True, True).then_inc(sem.mm_w, 1)
+    te.wait_ge(sem.wm_rdy, CB)
+    te.wait_ge(sem.l_rdy, 1)
+    for c in range(CB):
+        te.matmul(T.ps_y[:, blk[c]], T.v_sb[:, blk[c]], T.wm_sb[:, blk[c]], True, c == 0).then_inc(sem.mm_y, 1)
+        if c:
+            te.matmul(T.ps_y[:, blk[c]], T.l_sb[:, blk[c - 1]], T.q_sb[:, blk[c]], False, True).then_inc(sem.mm_y, 1)
+
+    def engines(dst):
+        m = topo.mask(core, cores[dst[0]])
+        for d in dst:
+            m &= topo.mask(core, cores[d])
+        return m
+
+    def count(m):
+        return bin(m).count("1")
+
+    got = {}
+    for r in range(N):
+        for (_, dst, slot) in calls[r]:
+            if rank in dst:
+                m = topo.mask(cores[r], cores[dst[0]])
+                for d in dst:
+                    m &= topo.mask(cores[r], cores[d])
+                got[slot] = count(m)
+
+    for n, slot in enumerate(zp):
+        te.wait_ge(sem["arr%d" % slot], got[slot])
+        te.matmul(T.ps_z[:, 0:W], T["land%d" % slot][:], T.q_sb[:], n == 0, n == len(zp) - 1).then_inc(sem.mm_z, 1)
+
+    if mine:
+        ve.wait_ge(sem.mm_s, CB)
+        ve.tensor_copy(T.s_sb[:], T.ps_s[:, 0:B]).then_inc(sem.s_rdy, 1)
+    ve.wait_ge(sem.mm_l, 3)
+    ve.tensor_copy(T.l_sb[:], T.ps_l[:, 0:2 * B]).then_inc(sem.l_rdy, 1)
+    ve.wait_ge(sem.mm_w, CB)
+    ve.wait_ge(sem.ld_m, 16)
+    for c in range(CB):
+        ve.tensor_tensor(T.wm_sb[:, blk[c]], T.ps_w[:, blk[c]], T.m_sb[:], AluOpType.mult).then_inc(sem.wm_rdy, 1)
+    ve.wait_ge(sem.mm_y, 2 * CB - 1)
+    if zp:
+        ve.tensor_copy(T.yl_sb[:], T.ps_y[:, 0:W]).then_inc(sem.yl_rdy, 1)
+        ve.wait_ge(sem.yl_rdy, 1)
+        ve.wait_ge(sem.mm_z, len(zp))
+        ve.tensor_tensor(T.y_sb[:], T.ps_z[:, 0:W], T.yl_sb[:], AluOpType.add).then_inc(sem.y_rdy, 1)
+    else:
+        ve.tensor_copy(T.y_sb[:], T.ps_y[:, 0:W]).then_inc(sem.y_rdy, 1)
+
+    sy.wait_ge(sem.y_rdy, 1)
+    sy.dma_start(T.y[:], T.y_sb[:]).then_inc(sem.stored, 16)
+    sy.wait_ge(sem.stored, 16)
+
+    waited = set(zp)
+    left = 0
+    if mine:
+        g.wait_ge(sem.s_rdy, 1)
+    for (need, dst, slot) in mine:
+        for p in need:
+            g.wait_ge(sem["arr%d" % p], got[p])
+            waited.add(p)
+        m = engines(dst)
+        ids = []
+        for d in dst:
+            rid, pid = topo.addr(cores[d], core)
+            ids.append(DstId(rid=rid, pnc=pid))
+        srcs = [T.s_sb[:]] + [T["land%d" % p][:] for p in need]
+        tr = RemoteDMATransfer(dst_ids=ids, dma_engine_mask=m, remote_sem=sem["arr%d" % slot], srcs=srcs,
+                               dsts=[T["land%d" % slot][:] for _ in dst], alu_op=1 if need else 0)
+        g.remote_dma_fused([tr], local_sem=sem.sent)
+        left += count(m)
+    if left:
+        g.wait_ge(sem.sent, left)
+    for p in got:
+        if p not in waited:
+            g.wait_ge(sem["arr%d" % p], got[p])

@@ -3,9 +3,9 @@ from concourse.mybir import AluOpType
 
 N, CB, B = 12, 3, 128
 W = CB * B
-GS = 4
+GS = 3
 NG = N // GS
-NLAND = GS + NG - 1
+NLAND = 2 * GS + NG - 1
 
 SCRATCH = {
     "kt_sb": ("sbuf", [B, W], "bfloat16"),
@@ -16,40 +16,71 @@ SCRATCH = {
     "s_sb": ("sbuf", [B, B], "bfloat16"),
     "l_sb": ("sbuf", [B, 2 * B], "bfloat16"),
     "wm_sb": ("sbuf", [B, W], "bfloat16"),
-    "yl_sb": ("sbuf", [B, W], "float32"),
     "y_sb": ("sbuf", [B, W], "bfloat16"),
     "ps_s": ("psum", [B, 512], "float32"),
     "ps_l": ("psum", [B, 512], "float32"),
     "ps_w": ("psum", [B, 512], "float32"),
-    "ps_y": ("psum", [B, 512], "float32"),
-    "ps_z": ("psum", [B, 512], "float32"),
 }
+for _i in range(CB):
+    SCRATCH["ps_y%d" % _i] = ("psum", [B, 512], "float32")
 for _i in range(NLAND):
     SCRATCH["land%d" % _i] = ("sbuf", [B, B], "bfloat16")
 
-SEMAPHORES = ["ld_kt", "ld_v", "ld_q", "ld_k", "ld_m", "mm_s", "mm_l", "mm_w", "mm_y", "mm_z",
-              "s_rdy", "l_rdy", "wm_rdy", "yl_rdy", "y_rdy", "sent", "stored"] + ["arr%d" % _i for _i in range(NLAND)]
+SEMAPHORES = (["ld_kt", "ld_v", "ld_q", "ld_k", "ld_m", "mm_s", "mm_l", "mm_w", "s_rdy", "l_rdy", "wm_rdy", "y_rdy",
+               "sent", "stored"] + ["fin%d" % _i for _i in range(CB)] + ["arr%d" % _i for _i in range(NLAND)])
+
+
+def _perms(n):
+    if n == 0:
+        return [[]]
+    out = []
+    for p in _perms(n - 1):
+        for i in range(n):
+            out.append(p[:i] + [n - 1] + p[i:])
+    return out
+
+
+def _match(src, dst, cores, topo):
+    best, bc = None, None
+    for p in _perms(len(dst)):
+        if not all(topo.may_write(cores[s], cores[dst[p[i]]]) for i, s in enumerate(src)):
+            continue
+        c = sum(0 if (topo.same_plane(cores[s], cores[dst[p[i]]]) or topo.mates(cores[s], cores[dst[p[i]]])) else 1
+                for i, s in enumerate(src))
+        if bc is None or c < bc:
+            best, bc = [dst[p[i]] for i in range(len(src))], c
+    return best
 
 
 def plan(cores, topo):
+    grp = [list(range(j * GS, (j + 1) * GS)) for j in range(NG)]
     calls = [[] for _ in range(N)]
-    pieces = [[] for _ in range(N)]
-    for j in range(NG):
-        mem = list(range(j * GS, (j + 1) * GS))
-        later = list(range((j + 1) * GS, N))
-        share = {r: [] for r in mem}
-        for d in later:
-            own = [r for r in mem if topo.same_plane(cores[r], cores[d])]
-            cand = own if own else [r for r in mem if topo.may_write(cores[r], cores[d])]
-            share[min(cand, key=lambda r: len(share[r]))].append(d)
+    when = [[] for _ in range(N)]
+    for j, mem in enumerate(grp):
+        later = grp[j + 1:]
+        raw0 = GS if j == NG - 1 else 0
+        direct = later[-1] if len(later) > 2 else []
+        served = later[:-1] if direct else later
+        folds = [_match(mem, dg, cores, topo) for dg in reversed(served)]
         for i, r in enumerate(mem):
             dst = [mem[(i + t) % GS] for t in range(1, GS)]
-            dst = [d for d in dst if d > r or share[d]]
+            if not later:
+                dst = [d for d in dst if d > r]
+            for n, d in enumerate(dst):
+                if d > r:
+                    when[d].append((n, raw0 + i))
+            for t in range(len(direct)):
+                d = direct[(i + t) % GS]
+                when[d].append((len(dst), raw0 + i))
+                dst = dst + [d]
             if dst:
-                calls[r].append(([], dst, i))
-            if share[r]:
-                calls[r].append(([p for p in range(GS) if p != i], share[r], GS + j))
-            pieces[r] = [p for p in range(i - 1, -1, -1)] + [GS + jj for jj in range(j - 1, -1, -1)]
+                calls[r].append(([], dst, raw0 + i))
+            fd = [f[i] for f in folds]
+            if fd:
+                calls[r].append(([raw0 + p for p in range(GS) if p != i], fd, 2 * GS + j))
+                for n, d in enumerate(fd):
+                    when[d].append((100 + n, 2 * GS + j))
+    pieces = [[s for (_, s) in sorted(w, key=lambda x: x[0])] for w in when]
     return calls, pieces
 
 
@@ -70,6 +101,21 @@ def rank_program(g, core, T, topo):
     sc.dma_start(T.k_sb[:], T.k[:]).then_inc(sem.ld_k, 16)
     sy.dma_start(T.m_sb[:], T.m[:]).then_inc(sem.ld_m, 16)
 
+    def engines(src, dst):
+        m = topo.mask(cores[src], cores[dst[0]])
+        for d in dst:
+            m &= topo.mask(cores[src], cores[d])
+        return m
+
+    def count(m):
+        return bin(m).count("1")
+
+    got = {}
+    for r in range(N):
+        for (_, dst, slot) in calls[r]:
+            if rank in dst:
+                got[slot] = count(engines(r, dst))
+
     te.wait_ge(sem.ld_kt, 16)
     te.wait_ge(sem.ld_v, 16)
     if mine:
@@ -84,32 +130,21 @@ def rank_program(g, core, T, topo):
         te.matmul(T.ps_w[:, blk[c]], T.k_sb[:, blk[c]], T.q_sb[:, blk[c]], True, True).then_inc(sem.mm_w, 1)
     te.wait_ge(sem.wm_rdy, CB)
     te.wait_ge(sem.l_rdy, 1)
+    total = [1 + (1 if c else 0) + len(zp) for c in range(CB)]
+    done = [0] * CB
+
+    def enter(c, lhsT, rhs):
+        done[c] += 1
+        te.matmul(T["ps_y%d" % c][:, 0:B], lhsT, rhs, done[c] == 1, done[c] == total[c]).then_inc(sem["fin%d" % c], 1)
+
     for c in range(CB):
-        te.matmul(T.ps_y[:, blk[c]], T.v_sb[:, blk[c]], T.wm_sb[:, blk[c]], True, c == 0).then_inc(sem.mm_y, 1)
+        enter(c, T.v_sb[:, blk[c]], T.wm_sb[:, blk[c]])
         if c:
-            te.matmul(T.ps_y[:, blk[c]], T.l_sb[:, blk[c - 1]], T.q_sb[:, blk[c]], False, True).then_inc(sem.mm_y, 1)
-
-    def engines(dst):
-        m = topo.mask(core, cores[dst[0]])
-        for d in dst:
-            m &= topo.mask(core, cores[d])
-        return m
-
-    def count(m):
-        return bin(m).count("1")
-
-    got = {}
-    for r in range(N):
-        for (_, dst, slot) in calls[r]:
-            if rank in dst:
-                m = topo.mask(cores[r], cores[dst[0]])
-                for d in dst:
-                    m &= topo.mask(cores[r], cores[d])
-                got[slot] = count(m)
-
-    for n, slot in enumerate(zp):
+            enter(c, T.l_sb[:, blk[c - 1]], T.q_sb[:, blk[c]])
+    for slot in zp:
         te.wait_ge(sem["arr%d" % slot], got[slot])
-        te.matmul(T.ps_z[:, 0:W], T["land%d" % slot][:], T.q_sb[:], n == 0, n == len(zp) - 1).then_inc(sem.mm_z, 1)
+        for c in range(CB):
+            enter(c, T["land%d" % slot][:], T.q_sb[:, blk[c]])
 
     if mine:
         ve.wait_ge(sem.mm_s, CB)
@@ -120,16 +155,11 @@ def rank_program(g, core, T, topo):
     ve.wait_ge(sem.ld_m, 16)
     for c in range(CB):
         ve.tensor_tensor(T.wm_sb[:, blk[c]], T.ps_w[:, blk[c]], T.m_sb[:], AluOpType.mult).then_inc(sem.wm_rdy, 1)
-    ve.wait_ge(sem.mm_y, 2 * CB - 1)
-    if zp:
-        ve.tensor_copy(T.yl_sb[:], T.ps_y[:, 0:W]).then_inc(sem.yl_rdy, 1)
-        ve.wait_ge(sem.yl_rdy, 1)
-        ve.wait_ge(sem.mm_z, len(zp))
-        ve.tensor_tensor(T.y_sb[:], T.ps_z[:, 0:W], T.yl_sb[:], AluOpType.add).then_inc(sem.y_rdy, 1)
-    else:
-        ve.tensor_copy(T.y_sb[:], T.ps_y[:, 0:W]).then_inc(sem.y_rdy, 1)
+    for c in range(CB):
+        ve.wait_ge(sem["fin%d" % c], total[c])
+        ve.tensor_copy(T.y_sb[:, blk[c]], T["ps_y%d" % c][:, 0:B]).then_inc(sem.y_rdy, 1)
 
-    sy.wait_ge(sem.y_rdy, 1)
+    sy.wait_ge(sem.y_rdy, CB)
     sy.dma_start(T.y[:], T.y_sb[:]).then_inc(sem.stored, 16)
     sy.wait_ge(sem.stored, 16)
 
@@ -141,7 +171,7 @@ def rank_program(g, core, T, topo):
         for p in need:
             g.wait_ge(sem["arr%d" % p], got[p])
             waited.add(p)
-        m = engines(dst)
+        m = engines(rank, dst)
         ids = []
         for d in dst:
             rid, pid = topo.addr(cores[d], core)

@@ -17,6 +17,8 @@ SCRATCH = {
     "l_sb": ("sbuf", [B, 2 * B], "bfloat16"),
     "wm_sb": ("sbuf", [B, W], "bfloat16"),
     "y_sb": ("sbuf", [B, W], "bfloat16"),
+    "mh_out": ("dram", [B, B // 2], "bfloat16"),
+    "mh_in": ("dram", [B, B // 2], "bfloat16"),
     "ps_s": ("psum", [B, 512], "float32"),
     "ps_l": ("psum", [B, 512], "float32"),
     "ps_w": ("psum", [B, 512], "float32"),
@@ -26,8 +28,9 @@ for _i in range(CB):
 for _i in range(NLAND):
     SCRATCH["land%d" % _i] = ("sbuf", [B, B], "bfloat16")
 
-SEMAPHORES = (["ld_kt", "ld_v", "ld_q", "ld_k", "ld_m", "mm_s", "mm_l", "mm_w", "s_rdy", "l_rdy", "wm_rdy", "y_rdy",
-               "sent", "stored"] + ["fin%d" % _i for _i in range(CB)] + ["arr%d" % _i for _i in range(NLAND)])
+SEMAPHORES = (["ld_kt", "ld_v", "ld_q", "ld_k", "ld_m", "ld_mh", "ld_m2", "arr_m", "mm_s", "mm_l", "mm_w", "s_rdy", "l_rdy",
+               "wm_rdy", "y_rdy", "sent", "stored"] + ["fin%d" % _i for _i in range(CB)]
+              + ["arr%d" % _i for _i in range(NLAND)])
 
 
 def _perms(n):
@@ -81,7 +84,8 @@ def plan(cores, topo):
                 for n, d in enumerate(fd):
                     when[d].append((100 + n, 2 * GS + j))
     pieces = [[s for (_, s) in sorted(w, key=lambda x: x[0])] for w in when]
-    return calls, pieces
+    early = [len([1 for (t, _) in w if t < 100]) for w in when]
+    return calls, pieces, early
 
 
 def rank_program(g, core, T, topo):
@@ -89,17 +93,26 @@ def rank_program(g, core, T, topo):
     if rank is None:
         return
     cores = T.cores
-    calls, pieces = plan(cores, topo)
-    mine, zp = calls[rank], pieces[rank]
+    calls, pieces, early = plan(cores, topo)
+    mine, zp, ne = calls[rank], pieces[rank], early[rank]
     sem = T.sem
     te, ve, sy, sc = g.tensor, g.vector, g.sync, g.scalar
     blk = [slice(B * c, B * c + B) for c in range(CB)]
 
+    mate = [p for p in range(N) if p != rank and topo.mates(core, cores[p]) and topo.may_write(core, cores[p])
+            and topo.may_write(cores[p], core)]
+    mate = mate[0] if mate else None
+    H = B // 2
+    own = slice(0, B) if mate is None else (slice(0, H) if rank < mate else slice(H, B))
+    oth = None if mate is None else (slice(H, B) if rank < mate else slice(0, H))
+
+    if mate is not None:
+        sy.dma_start(T.mh_out[:], T.m[own, :]).then_inc(sem.ld_mh, 16)
     sy.dma_start(T.kt_sb[:], T.kt[:]).then_inc(sem.ld_kt, 16)
     sc.dma_start(T.v_sb[:], T.v[:]).then_inc(sem.ld_v, 16)
     sy.dma_start(T.q_sb[:], T.q[:]).then_inc(sem.ld_q, 16)
     sc.dma_start(T.k_sb[:], T.k[:]).then_inc(sem.ld_k, 16)
-    sy.dma_start(T.m_sb[:], T.m[:]).then_inc(sem.ld_m, 16)
+    sy.dma_start(T.m_sb[own, :], T.m[own, :]).then_inc(sem.ld_m, 16)
 
     def engines(src, dst):
         m = topo.mask(cores[src], cores[dst[0]])
@@ -109,6 +122,10 @@ def rank_program(g, core, T, topo):
 
     def count(m):
         return bin(m).count("1")
+
+    if mate is not None:
+        sc.wait_ge(sem.arr_m, count(engines(mate, [rank])))
+        sc.dma_start(T.m_sb[oth, :], T.mh_in[:]).then_inc(sem.ld_m2, 16)
 
     got = {}
     for r in range(N):
@@ -128,7 +145,6 @@ def rank_program(g, core, T, topo):
     te.wait_ge(sem.ld_k, 16)
     for c in range(CB):
         te.matmul(T.ps_w[:, blk[c]], T.k_sb[:, blk[c]], T.q_sb[:, blk[c]], True, True).then_inc(sem.mm_w, 1)
-    te.wait_ge(sem.wm_rdy, CB)
     te.wait_ge(sem.l_rdy, 1)
     total = [1 + (1 if c else 0) + len(zp) for c in range(CB)]
     done = [0] * CB
@@ -137,14 +153,19 @@ def rank_program(g, core, T, topo):
         done[c] += 1
         te.matmul(T["ps_y%d" % c][:, 0:B], lhsT, rhs, done[c] == 1, done[c] == total[c]).then_inc(sem["fin%d" % c], 1)
 
+    def pieces_in(slots):
+        for slot in slots:
+            te.wait_ge(sem["arr%d" % slot], got[slot])
+            for c in range(CB):
+                enter(c, T["land%d" % slot][:], T.q_sb[:, blk[c]])
+
+    for c in range(1, CB):
+        enter(c, T.l_sb[:, blk[c - 1]], T.q_sb[:, blk[c]])
+    pieces_in(zp[:ne])
+    te.wait_ge(sem.wm_rdy, CB)
     for c in range(CB):
         enter(c, T.v_sb[:, blk[c]], T.wm_sb[:, blk[c]])
-        if c:
-            enter(c, T.l_sb[:, blk[c - 1]], T.q_sb[:, blk[c]])
-    for slot in zp:
-        te.wait_ge(sem["arr%d" % slot], got[slot])
-        for c in range(CB):
-            enter(c, T["land%d" % slot][:], T.q_sb[:, blk[c]])
+    pieces_in(zp[ne:])
 
     if mine:
         ve.wait_ge(sem.mm_s, CB)
@@ -153,6 +174,8 @@ def rank_program(g, core, T, topo):
     ve.tensor_copy(T.l_sb[:], T.ps_l[:, 0:2 * B]).then_inc(sem.l_rdy, 1)
     ve.wait_ge(sem.mm_w, CB)
     ve.wait_ge(sem.ld_m, 16)
+    if mate is not None:
+        ve.wait_ge(sem.ld_m2, 16)
     for c in range(CB):
         ve.tensor_tensor(T.wm_sb[:, blk[c]], T.ps_w[:, blk[c]], T.m_sb[:], AluOpType.mult).then_inc(sem.wm_rdy, 1)
     for c in range(CB):
@@ -165,6 +188,13 @@ def rank_program(g, core, T, topo):
 
     waited = set(zp)
     left = 0
+    if mate is not None:
+        mm = engines(rank, [mate])
+        rid, pid = topo.addr(cores[mate], core)
+        g.wait_ge(sem.ld_mh, 16)
+        g.remote_dma_fused([RemoteDMATransfer(dst_ids=[DstId(rid=rid, pnc=pid)], dma_engine_mask=mm, remote_sem=sem.arr_m,
+                                              srcs=[T.mh_out[:]], dsts=[T.mh_in[:]], alu_op=0)], local_sem=sem.sent)
+        left += count(mm)
     if mine:
         g.wait_ge(sem.s_rdy, 1)
     for (need, dst, slot) in mine:

from concourse.bass import DstId, RemoteDMATransfer
from concourse.mybir import AluOpType

N, CB, B = 12, 3, 128
W = CB * B
GS = 3
NG = N // GS
NLAND = 2 * GS + NG - 1

SCRATCH = {
    "kt_sb": ("sbuf", [B, W], "bfloat16"),
    "v_sb": ("sbuf", [B, W], "bfloat16"),
    "q_sb": ("sbuf", [B, W], "bfloat16"),
    "k_sb": ("sbuf", [B, W], "bfloat16"),
    "m_sb": ("sbuf", [B, B], "bfloat16"),
    "s_sb": ("sbuf", [B, B], "bfloat16"),
    "l_sb": ("sbuf", [B, 2 * B], "bfloat16"),
    "wm_sb": ("sbuf", [B, W], "bfloat16"),
    "y_sb": ("sbuf", [B, W], "bfloat16"),
    "mh_out": ("dram", [B, B // 2], "bfloat16"),
    "mh_in": ("dram", [B, B // 2], "bfloat16"),
    "ps_s": ("psum", [B, 512], "float32"),
    "ps_l": ("psum", [B, 512], "float32"),
    "ps_w": ("psum", [B, 512], "float32"),
}
for _i in range(CB):
    SCRATCH["ps_y%d" % _i] = ("psum", [B, 512], "float32")
for _i in range(NLAND):
    SCRATCH["land%d" % _i] = ("sbuf", [B, B], "bfloat16")

SEMAPHORES = (["ld_kt", "ld_v", "ld_q", "ld_k", "ld_m", "ld_mh", "ld_m2", "arr_m", "mm_s", "mm_l", "mm_w", "s_rdy", "l_rdy",
               "wm_rdy", "y_rdy", "sent", "stored"] + ["fin%d" % _i for _i in range(CB)]
              + ["arr%d" % _i for _i in range(NLAND)])


def _perms(n):
    if n == 0:
        return [[]]
    out = []
    for p in _perms(n - 1):
        for i in range(n):
            out.append(p[:i] + [n - 1] + p[i:])
    return out


def _match(src, dst, cores, topo):
    best, bc = None, None
    for p in _perms(len(dst)):
        if not all(topo.may_write(cores[s], cores[dst[p[i]]]) for i, s in enumerate(src)):
            continue
        c = sum(0 if (topo.same_plane(cores[s], cores[dst[p[i]]]) or topo.mates(cores[s], cores[dst[p[i]]])) else 1
                for i, s in enumerate(src))
        if bc is None or c < bc:
            best, bc = [dst[p[i]] for i in range(len(src))], c
    return best


def plan(cores, topo):
    grp = [list(range(j * GS, (j + 1) * GS)) for j in range(NG)]
    calls = [[] for _ in range(N)]
    when = [[] for _ in range(N)]
    for j, mem in enumerate(grp):
        later = grp[j + 1:]
        raw0 = GS if j == NG - 1 else 0
        direct = later[-1] if len(later) > 2 else []
        served = later[:-1] if direct else later
        folds = [_match(mem, dg, cores, topo) for dg in reversed(served)]
        for i, r in enumerate(mem):
            dst = [mem[(i + t) % GS] for t in range(1, GS)]
            if not later:
                dst = [d for d in dst if d > r]
            for n, d in enumerate(dst):
                if d > r:
                    when[d].append((n, raw0 + i))
            for t in range(len(direct)):
                d = direct[(i + t) % GS]
                when[d].append((len(dst), raw0 + i))
                dst = dst + [d]
            if dst:
                calls[r].append(([], dst, raw0 + i))
            fd = [f[i] for f in folds]
            if fd:
                calls[r].append(([raw0 + p for p in range(GS) if p != i], fd, 2 * GS + j))
                for n, d in enumerate(fd):
                    when[d].append((100 + n, 2 * GS + j))
    pieces = [[s for (_, s) in sorted(w, key=lambda x: x[0])] for w in when]
    early = [len([1 for (t, _) in w if t < 100]) for w in when]
    return calls, pieces, early


def rank_program(g, core, T, topo):
    rank = T.rank_of(core)
    if rank is None:
        return
    cores = T.cores
    calls, pieces, early = plan(cores, topo)
    mine, zp, ne = calls[rank], pieces[rank], early[rank]
    sem = T.sem
    te, ve, sy, sc = g.tensor, g.vector, g.sync, g.scalar
    blk = [slice(B * c, B * c + B) for c in range(CB)]

    mate = [p for p in range(N) if p != rank and topo.mates(core, cores[p]) and topo.may_write(core, cores[p])
            and topo.may_write(cores[p], core)]
    mate = mate[0] if mate else None
    H = B // 2
    own = slice(0, B) if mate is None else (slice(0, H) if rank < mate else slice(H, B))
    oth = None if mate is None else (slice(H, B) if rank < mate else slice(0, H))

    if mate is not None:
        sy.dma_start(T.mh_out[:], T.m[own, :]).then_inc(sem.ld_mh, 16)
    sy.dma_start(T.kt_sb[:], T.kt[:]).then_inc(sem.ld_kt, 16)
    sc.dma_start(T.v_sb[:], T.v[:]).then_inc(sem.ld_v, 16)
    sy.dma_start(T.q_sb[:], T.q[:]).then_inc(sem.ld_q, 16)
    sc.dma_start(T.k_sb[:], T.k[:]).then_inc(sem.ld_k, 16)
    sy.dma_start(T.m_sb[own, :], T.m[own, :]).then_inc(sem.ld_m, 16)

    def engines(src, dst):
        m = topo.mask(cores[src], cores[dst[0]])
        for d in dst:
            m &= topo.mask(cores[src], cores[d])
        return m

    def count(m):
        return bin(m).count("1")

    if mate is not None:
        sc.wait_ge(sem.arr_m, count(engines(mate, [rank])))
        sc.dma_start(T.m_sb[oth, :], T.mh_in[:]).then_inc(sem.ld_m2, 16)

    got = {}
    for r in range(N):
        for (_, dst, slot) in calls[r]:
            if rank in dst:
                got[slot] = count(engines(r, dst))

    te.wait_ge(sem.ld_kt, 16)
    te.wait_ge(sem.ld_v, 16)
    if mine:
        for c in range(CB):
            te.matmul(T.ps_s[:, 0:B], T.kt_sb[:, blk[c]], T.v_sb[:, blk[c]], c == 0, c == CB - 1).then_inc(sem.mm_s, 1)
    te.matmul(T.ps_l[:, 0:B], T.kt_sb[:, blk[0]], T.v_sb[:, blk[0]], True, True).then_inc(sem.mm_l, 1)
    te.matmul(T.ps_l[:, B:2 * B], T.kt_sb[:, blk[0]], T.v_sb[:, blk[0]], True, False).then_inc(sem.mm_l, 1)
    te.matmul(T.ps_l[:, B:2 * B], T.kt_sb[:, blk[1]], T.v_sb[:, blk[1]], False, True).then_inc(sem.mm_l, 1)
    te.wait_ge(sem.ld_q, 16)
    te.wait_ge(sem.ld_k, 16)
    for c in range(CB):
        te.matmul(T.ps_w[:, blk[c]], T.k_sb[:, blk[c]], T.q_sb[:, blk[c]], True, True).then_inc(sem.mm_w, 1)
    te.wait_ge(sem.l_rdy, 1)
    total = [1 + (1 if c else 0) + len(zp) for c in range(CB)]
    done = [0] * CB

    def enter(c, lhsT, rhs):
        done[c] += 1
        te.matmul(T["ps_y%d" % c][:, 0:B], lhsT, rhs, done[c] == 1, done[c] == total[c]).then_inc(sem["fin%d" % c], 1)

    def pieces_in(slots):
        for slot in slots:
            te.wait_ge(sem["arr%d" % slot], got[slot])
            for c in range(CB):
                enter(c, T["land%d" % slot][:], T.q_sb[:, blk[c]])

    for c in range(1, CB):
        enter(c, T.l_sb[:, blk[c - 1]], T.q_sb[:, blk[c]])
    pieces_in(zp[:ne])
    te.wait_ge(sem.wm_rdy, CB)
    for c in range(CB):
        enter(c, T.v_sb[:, blk[c]], T.wm_sb[:, blk[c]])
    pieces_in(zp[ne:])

    if mine:
        ve.wait_ge(sem.mm_s, CB)
        ve.tensor_copy(T.s_sb[:], T.ps_s[:, 0:B]).then_inc(sem.s_rdy, 1)
    ve.wait_ge(sem.mm_l, 3)
    ve.tensor_copy(T.l_sb[:], T.ps_l[:, 0:2 * B]).then_inc(sem.l_rdy, 1)
    ve.wait_ge(sem.mm_w, CB)
    ve.wait_ge(sem.ld_m, 16)
    if mate is not None:
        ve.wait_ge(sem.ld_m2, 16)
    for c in range(CB):
        ve.tensor_tensor(T.wm_sb[:, blk[c]], T.ps_w[:, blk[c]], T.m_sb[:], AluOpType.mult).then_inc(sem.wm_rdy, 1)
    for c in range(CB):
        ve.wait_ge(sem["fin%d" % c], total[c])
        ve.tensor_copy(T.y_sb[:, blk[c]], T["ps_y%d" % c][:, 0:B]).then_inc(sem.y_rdy, 1)

    sy.wait_ge(sem.y_rdy, CB)
    sy.dma_start(T.y[:], T.y_sb[:]).then_inc(sem.stored, 16)
    sy.wait_ge(sem.stored, 16)

    waited = set(zp)
    left = 0
    if mate is not None:
        mm = engines(rank, [mate])
        rid, pid = topo.addr(cores[mate], core)
        g.wait_ge(sem.ld_mh, 16)
        g.remote_dma_fused([RemoteDMATransfer(dst_ids=[DstId(rid=rid, pnc=pid)], dma_engine_mask=mm, remote_sem=sem.arr_m,
                                              srcs=[T.mh_out[:]], dsts=[T.mh_in[:]], alu_op=0)], local_sem=sem.sent)
        left += count(mm)
    if mine:
        g.wait_ge(sem.s_rdy, 1)
    for (need, dst, slot) in mine:
        for p in need:
            g.wait_ge(sem["arr%d" % p], got[p])
            waited.add(p)
        m = engines(rank, dst)
        ids = []
        for d in dst:
            rid, pid = topo.addr(cores[d], core)
            ids.append(DstId(rid=rid, pnc=pid))
        srcs = [T.s_sb[:]] + [T["land%d" % p][:] for p in need]
        tr = RemoteDMATransfer(dst_ids=ids, dma_engine_mask=m, remote_sem=sem["arr%d" % slot], srcs=srcs,
                               dsts=[T["land%d" % slot][:] for _ in dst], alu_op=1 if need else 0)
        g.remote_dma_fused([tr], local_sem=sem.sent)
        left += count(m)
    if left:
        g.wait_ge(sem.sent, left)
    for p in got:
        if p not in waited:
            g.wait_ge(sem["arr%d" % p], got[p])
